import numpy as np
import ml_dtypes


def mxq(x, axis, fmt="e4m3"):
    dtype, down = {"e4m3": (ml_dtypes.float8_e4m3fn, 7), "e5m2": (ml_dtypes.float8_e5m2, 14)}[fmt]
    v = np.moveaxis(np.asarray(x, np.float32).astype(ml_dtypes.bfloat16).astype(np.float64), axis, -1)
    blocks = v.reshape(v.shape[:-1] + (-1, 32))
    amax = np.abs(blocks).max(-1, keepdims=True)
    byte = np.maximum(np.where(amax > 0, np.frexp(amax)[1] - 1 + 127, 0) - down, 1)
    scale = np.exp2(byte - 127.0)
    codes = (blocks / scale).astype(np.float32).astype(dtype).astype(np.float64)
    return np.moveaxis((codes * scale).reshape(v.shape), -1, axis)


WIDE = False


def mx_kscale(k):
    if not WIDE:
        return np.ones(k)
    levels = np.array([10, -10, 5, -5, 0])
    if k % 512:
        return np.exp2(np.random.permutation(np.resize(levels, k // 32))).repeat(32)
    a = np.empty((k // 512, 16))
    for p in range(k // 512):
        a[p, :8] = np.random.permutation(np.resize(levels, 8))
        for g in range(8):
            far = levels[np.abs(levels - a[p, g]) >= 10]
            a[p, g + 8] = far[np.random.randint(len(far))]
    return np.exp2(a.ravel()).repeat(32)


def f64(x):
    return np.asarray(x).astype(np.float64)


def striped(idx):
    return np.tile(idx.reshape(-1, 16).T, (8, 1)).astype(np.uint16)


def unstriped(offs):
    return offs[:16].T.reshape(-1).astype(np.int64)


def striped8(idx):
    return np.concatenate([x.reshape(-1, 16).T for x in idx]).astype(np.uint16)


def runs(offs, k):
    lists = np.stack([offs[16 * r : 16 * r + 16].T.reshape(-1) for r in range(8)]).astype(np.int64)
    return lists[np.arange(k) % 512 // 64]


def pack_weight(w):
    k, n = w.shape
    w = f64(np.asarray(w, np.float32).astype(ml_dtypes.bfloat16)).reshape(k // 32, 32, n)
    amax = np.abs(w).max(1)
    byte = np.clip(np.where(amax > 0, np.frexp(amax)[1] - 1 + 127 - 7, 1), 1, 254)
    scaled = (w * np.exp2(127.0 - byte)[:, None, :]).reshape(k, n).astype(np.float32)
    words = np.ascontiguousarray(scaled.reshape(k // 512, 128, 4, n).transpose(0, 1, 3, 2)).astype(ml_dtypes.float8_e4m3fn).view(np.uint8)
    return words, np.ascontiguousarray(byte.astype(np.uint8).reshape(k // 512, 16, n))


def unpack_weight(words, scales):
    g, p, n, _ = words.shape
    vals = np.ascontiguousarray(words).view(ml_dtypes.float8_e4m3fn).astype(np.float64) * np.repeat(np.exp2(scales.astype(np.float64) - 127.0), 8, axis=1)[..., None]
    return vals.transpose(0, 1, 3, 2).reshape(g * 512, n)


def sigmoid(v):
    return 1.0 / (1.0 + np.exp(-np.maximum(v, -700.0)))

def planes(y):
    n, m = y.shape
    v = y.astype(np.float32).astype(ml_dtypes.bfloat16).astype(np.float64).reshape(n // 32, 32, m)
    top = np.abs(v).max(1)
    byte = np.clip(np.where(top > 0, np.frexp(top)[1] - 1 + 127 - 7, 1), 1, 254)
    codes = (v * np.exp2(127.0 - byte)[:, None, :]).reshape(n, m).astype(np.float32).astype(ml_dtypes.float8_e4m3fn).view(np.uint8)
    words = codes.reshape(n // 512, 128, 4, m).transpose(0, 1, 3, 2)
    return np.ascontiguousarray(words), np.ascontiguousarray(byte.astype(np.uint8).reshape(n // 512, 16, m))


K, T, S, V, N, H, U = 512, 2048, 512, 512, 512, 512, 1024


def setup_inputs():
    n = np.random.standard_normal
    s = mx_kscale(K)[:, None]
    u = mx_kscale(S)
    packed_xT = pack_weight(n((K, T)) * s)
    packed_w1 = pack_weight(n((K, H)) / np.sqrt(K) / s)
    packed_w2 = pack_weight(n((K, H)) / np.sqrt(K) / s)
    return {
        "x_words": packed_xT[0],
        "x_scales": packed_xT[1],
        "w1_words": packed_w1[0],
        "w1_scales": packed_w1[1],
        "w2_words": packed_w2[0],
        "w2_scales": packed_w2[1],
        "gk": (np.random.uniform(0.5, 1.5, (H, 1)) * u[:, None]).astype(np.float32),
        "gq": (np.random.uniform(0.5, 1.5, (H, 1)) / u[:, None]).astype(np.float32),
        "tab": n((S, U)).astype(np.float32),
        "wv": (n((K, N)) / np.sqrt(K) / s).astype(np.float32),
        "gi": (np.random.uniform(0.5, 1.5, (S, 1)) / u[:, None]).astype(np.float32),
        "gt": (np.random.uniform(0.5, 1.5, (S, 1)) * u[:, None]).astype(np.float32),
        "offs": striped(np.random.permutation(T)[:S]),
        "qs": striped(np.random.permutation(T)[:V]),
        "rel": striped8(np.random.randint(0, U, (8, V))),
    }


def reference(x_words, x_scales, w1_words, w1_scales, w2_words, w2_scales, gk, gq, tab, wv, gi, gt, offs, qs, rel):
    xq = unpack_weight(x_words, x_scales)[:, unstriped(offs)]
    val = xq.T @ mxq(f64(wv), 0, "e4m3")
    zv = f64(gi) * val
    kf = unpack_weight(w1_words, w1_scales).T @ xq
    z = f64(gk) * kf
    x_qs = unpack_weight(x_words, x_scales)[:, unstriped(qs)]
    qf = unpack_weight(w2_words, w2_scales).T @ x_qs
    z2 = f64(gq) * qf
    s = 0.0625 * ((mxq(z, 0, "e4m3").T @ mxq(z2, 0, "e4m3")))
    zp = f64(gt) * (sigmoid(s + f64(tab)[np.arange(S)[:, None], runs(rel, S)]))
    out_0 = 0.0625 * ((mxq(zv, 0, "e4m3").T @ mxq(zp, 0, "e4m3")))
    return (out_0,) + planes(out_0)

from contextlib import ExitStack

import concourse.mybir as mybir
from concourse.masks import make_identity

K, T, S, V, N, H, U = 512, 2048, 512, 512, 512, 512, 1024
FLOPS = 2 * 5 * 512 * 512 * 512

F32 = mybir.dt.float32
BF16 = mybir.dt.bfloat16
I32 = mybir.dt.int32
U32 = mybir.dt.uint32
U16 = mybir.dt.uint16
U8 = mybir.dt.uint8
FP8X4 = mybir.dt.float8_e4m3fn_x4
COPY = mybir.ActivationFunctionType.Copy
SIGMOID = mybir.ActivationFunctionType.Sigmoid
MULT = mybir.AluOpType.mult
ADD = mybir.AluOpType.add

P = 128
SLOTS = 4
BLOCKS = 16
RUN = 8
CHUNK = 128
CHUNKS = V // CHUNK
HALF = 256
SIXTEENTH = 0.0625


def tile_picked_listbias_sigmoid_po_kernel(
    tc, x_words, x_scales, w1_words, w1_scales, w2_words, w2_scales, gk, gq, tab, wv, gi, gt, offs, qs, rel, out_0, out_1, out_2
):
    nc = tc.nc
    with ExitStack() as ctx:
        keep = ctx.enter_context(tc.tile_pool(name="keep", bufs=1))
        ring = ctx.enter_context(tc.tile_pool(name="ring", bufs=2))
        psum = ctx.enter_context(tc.psum_pool(name="psum", bufs=8))

        def held(shape, dtype, name):
            return keep.tile(shape, dtype, name=name, align_bytes=64)

        def bank(shape, name):
            return psum.tile(shape, F32, name=name, tag="bank")

        def words_of(packed):
            return packed[0].rearrange("p n t -> p (n t)").bitcast(I32)

        def load_scale_rows(queue, plane, scales):
            for q in range(4):
                queue.dma_start(out=plane[32 * q : 32 * q + 4, :].bitcast(I32), in_=scales[0, 4 * q : 4 * q + 4, :].bitcast(I32))

        def deal(dst, src, width):
            nc.vector.tensor_copy(
                out=dst[:].bitcast(I32).rearrange("p (t b e) -> p t b e", t=SLOTS, e=width),
                in_=src[:].bitcast(I32).rearrange("p (b t e) -> p t b e", t=SLOTS, e=width),
            )

        def mx(out, lhs, lhs_scale, rhs, rhs_scale):
            nc.tensor.matmul_mx(
                out=out, lhsT=lhs.bitcast(FP8X4), lhsT_scale=lhs_scale, rhs=rhs.bitcast(FP8X4), rhs_scale=rhs_scale, start=True, stop=True
            )

        def quantize(codes, plane, values):
            nc.vector.quantize_mx(out=codes.bitcast(FP8X4), scales=plane, in_=values)

        def cols(i):
            return slice(P * i, P * (i + 1))

        offs_sb = keep.tile([P, S // 16], U16, name="offs_sb")
        qs_sb = keep.tile([P, V // 16], U16, name="qs_sb")
        rel_sb = keep.tile([P, V // 16], U16, name="rel_sb")
        x_plane = held([P, T], U8, "x_plane")
        x_sb = held([P, T], U32, "x_sb")
        w1_raw = held([P, H], U32, "w1_raw")
        w2_raw = held([P, H], U32, "w2_raw")
        w1_plane_raw = held([P, H], U8, "w1_plane_raw")
        w2_plane_raw = held([P, H], U8, "w2_plane_raw")
        gain_rows = [held([P, P], F32, "gain_rows%d" % i) for i in range(2)]
        ident = held([P, P], F32, "ident")
        wv_raw = held([P, SLOTS, N], F32, "wv_raw")
        tab_sb = [held([P, U], F32, "tab%d" % t) for t in range(SLOTS)]

        nc.vector.memset(x_plane[:].bitcast(I32), 0)
        nc.vector.memset(gain_rows[0][:], 0.0)
        nc.vector.memset(w1_plane_raw[:].bitcast(I32), 0)
        nc.vector.memset(w2_plane_raw[:].bitcast(I32), 0)
        nc.vector.memset(gain_rows[1][:], 0.0)

        tab_dealt = tab.rearrange("(b t e) u -> t b e u", t=SLOTS, e=RUN)
        nc.sync.dma_start(offs_sb[:], offs)
        nc.sync.dma_start(qs_sb[:], qs)
        load_scale_rows(nc.sync, x_plane, x_scales)
        nc.sync.dma_start(out=w1_raw[:].bitcast(I32), in_=words_of(w1_words))
        nc.sync.dma_start(out=x_sb[:].bitcast(I32), in_=words_of(x_words))
        load_scale_rows(nc.sync, w1_plane_raw, w1_scales)
        nc.sync.dma_start(rel_sb[:], rel)
        nc.sync.dma_start(out=w2_raw[:].bitcast(I32), in_=words_of(w2_words))
        nc.sync.dma_start(out=tab_sb[0][:], in_=tab_dealt[0])
        load_scale_rows(nc.sync, w2_plane_raw, w2_scales)
        nc.sync.dma_start(out=wv_raw[:], in_=wv.rearrange("(p j) n -> p j n", j=SLOTS))
        for t in range(1, SLOTS):
            nc.sync.dma_start(out=tab_sb[t][:], in_=tab_dealt[t])

        make_identity(nc, ident[:])
        for i, gain in enumerate((gk, gq, gi, gt)):
            nc.gpsimd.dma_start(
                out=gain_rows[i // 2][SLOTS * (i % 2) : SLOTS * (i % 2 + 1), :].rearrange("t (b e) -> t b e", e=RUN),
                in_=gain.rearrange("(b t e) o -> t b (e o)", t=SLOTS, e=RUN),
            )

        warm = held([P, 1], F32, "warm")
        nc.scalar.activation(out=warm[:], in_=ident[:, 0:1], func=SIGMOID)

        def turn_gains(i):
            turned = bank([P, P], "turned")
            nc.tensor.transpose(turned[:], gain_rows[i][:], ident[:])
            gains = held([P, 2 * SLOTS], F32, "gains%d" % i)
            nc.scalar.copy(out=gains[:], in_=turned[:, 0 : 2 * SLOTS])
            return gains[:, 0:SLOTS], gains[:, SLOTS : 2 * SLOTS]

        gk_sb, gq_sb = turn_gains(0)

        xk_plane_listed = held([P, S], U8, "xk_plane_listed")
        xk_plane = held([P, S], U8, "xk_plane")
        xq_plane = held([P, V], U8, "xq_plane")
        xk = held([P, S], U32, "xk")
        xq = held([P, V], U32, "xq")
        w1 = held([P, H], U32, "w1")
        w2 = held([P, H], U32, "w2")
        w1_plane = held([P, H], U8, "w1_plane")
        w2_plane = held([P, H], U8, "w2_plane")

        nc.vector.tensor_copy(out=xk_plane_listed[:], in_=x_plane[:].indirect(offs_sb[:]))
        nc.vector.tensor_copy(out=xq_plane[:], in_=x_plane[:].indirect(qs_sb[:]))
        deal(xk_plane, xk_plane_listed, RUN // 4)
        deal(w1, w1_raw, RUN)
        nc.vector.tensor_copy(out=xk[:].rearrange("p (t b e) -> p b t e", t=SLOTS, e=RUN), in_=x_sb[:].indirect(offs_sb[:]))
        deal(w1_plane, w1_plane_raw, RUN // 4)
        nc.vector.tensor_copy(out=xq[:], in_=x_sb[:].indirect(qs_sb[:]))
        deal(w2, w2_raw, RUN)
        deal(w2_plane, w2_plane_raw, RUN // 4)

        def weave_pairs(pairs, name):
            woven = held([P, SLOTS * 512], BF16, name + "_woven")
            nc.vector.tensor_copy(
                out=woven[:].bitcast(F32).rearrange("p (c u) -> p c u", u=2),
                in_=pairs[:].rearrange("p u c e -> p (u c e)").bitcast(F32).rearrange("p (u c) -> p c u", u=2),
            )
            codes = held([P, 512], U32, name)
            plane = held([P, 512], U8, name + "_plane")
            quantize(codes[:], plane[:], woven[:])
            return codes, plane

        z_pairs = held([P, 2, S, 2], BF16, "z_pairs")
        for t in range(SLOTS):
            kf = bank([P, S], "kf")
            mx(kf[:], w1[:, cols(t)], w1_plane[:, cols(t)], xk[:], xk_plane[:])
            nc.scalar.activation(out=z_pairs[:, t // 2, :, t % 2], in_=kf[:], func=COPY, scale=gk_sb[:, t : t + 1])

        bias = held([P, 2, SLOTS, HALF], F32, "bias")

        def gather_bias(h, t):
            nc.vector.tensor_copy(out=bias[:, h, t, :], in_=tab_sb[t][:].indirect(rel_sb[:, 16 * h : 16 * (h + 1)]))

        z2 = held([P, V], U32, "z2")
        z2_plane = held([P, V], U8, "z2_plane")

        def slotwise(gain):
            return gain.unsqueeze(1).to_broadcast([P, CHUNK, SLOTS])

        def queries(c):
            qf = bank([P, SLOTS, CHUNK], "qf")
            for t in range(SLOTS):
                mx(qf[:, t, :], w2[:, cols(t)], w2_plane[:, cols(t)], xq[:, cols(c)], xq_plane[:, cols(c)])
            woven = ring.tile([P, CHUNK, SLOTS], BF16, name="z2_woven", align_bytes=64)
            nc.vector.tensor_tensor(out=woven[:], in0=qf[:].rearrange("p t v -> p v t"), in1=slotwise(gq_sb), op=MULT)
            return woven

        def quantize_chunk(codes, plane, c, woven):
            quantize(codes[:, cols(c)], plane[:, cols(c)], woven[:].rearrange("p v t -> p (v t)"))

        gi_sb, gt_sb = turn_gains(1)
        gather_bias(0, 0)
        gather_bias(1, 0)
        woven0 = queries(0)
        woven1 = queries(1)
        quantize_chunk(z2, z2_plane, 0, woven0)
        quantize_chunk(z2, z2_plane, 1, woven1)
        z, z_plane = weave_pairs(z_pairs, "z")

        wv_woven = held([P, SLOTS * N], BF16, "wv_woven")
        nc.scalar.copy(
            out=wv_woven[:].rearrange("p (c i j) -> p c j i", i=4, j=SLOTS),
            in_=wv_raw[:].rearrange("p j (c i) -> p c j i", i=4),
        )
        for t in range(1, SLOTS):
            gather_bias(0, t)
        wvq = held([P, N], U32, "wvq")
        wvq_plane = held([P, N], U8, "wvq_plane")
        quantize(wvq[:], wvq_plane[:], wv_woven[:])

        def scores(c):
            s = bank([P, SLOTS, CHUNK], "s")
            for t in range(SLOTS):
                mx(s[:, t, :], z[:, cols(t)], z_plane[:, cols(t)], z2[:, cols(c)], z2_plane[:, cols(c)])
            logit = ring.tile([P, SLOTS, CHUNK], F32, name="logit")
            nc.vector.scalar_tensor_tensor(
                out=logit[:], in0=s[:], scalar=SIXTEENTH, in1=bias[:, c // 2, :, cols(c % 2)], op0=MULT, op1=ADD
            )
            sig = keep.tile([P, CHUNK, SLOTS], F32, name="sig%d" % c)
            nc.scalar.activation(
                out=sig[:].rearrange("p (c i) t -> p c t i", i=4), in_=logit[:].rearrange("p t (c i) -> p c t i", i=4), func=SIGMOID
            )
            return sig

        sigs = [scores(0), scores(1)]

        zv_pairs = held([P, 2, N, 2], BF16, "zv_pairs")
        for t in range(SLOTS):
            val = bank([P, N], "val")
            mx(val[:], xk[:, cols(t)], xk_plane[:, cols(t)], wvq[:], wvq_plane[:])
            nc.scalar.activation(
                out=zv_pairs[:, t // 2, :, t % 2].rearrange("p (j m) -> p j m", j=SLOTS),
                in_=val[:].rearrange("p (m j) -> p j m", j=SLOTS),
                func=COPY,
                scale=gi_sb[:, t : t + 1],
            )

        woven2 = queries(2)
        woven3 = queries(3)
        quantize_chunk(z2, z2_plane, 2, woven2)
        quantize_chunk(z2, z2_plane, 3, woven3)
        for t in range(1, SLOTS):
            gather_bias(1, t)
        zv, zv_plane = weave_pairs(zv_pairs, "zv")

        zp = held([P, V], U32, "zp")
        zp_plane = held([P, V], U8, "zp_plane")
        y_codes = held([P, V], U32, "y_codes")
        y_plane = held([P, V], U8, "y_plane")
        out_rows = out_0.rearrange("(p j) v -> p j v", j=SLOTS)

        def weights(c):
            woven = ring.tile([P, CHUNK, SLOTS], BF16, name="zp_woven", align_bytes=64)
            nc.vector.tensor_tensor(out=woven[:], in0=sigs[c][:], in1=slotwise(gt_sb), op=MULT)
            return woven

        def result(c):
            acc = bank([P, SLOTS, CHUNK], "acc")
            for j in range(SLOTS):
                mx(acc[:, j, :], zv[:, cols(j)], zv_plane[:, cols(j)], zp[:, cols(c)], zp_plane[:, cols(c)])
            woven = ring.tile([P, CHUNK, SLOTS], BF16, name="y_woven", align_bytes=64)
            nc.scalar.activation(out=woven[:], in_=acc[:].rearrange("p j v -> p v j"), func=COPY, scale=SIXTEENTH)
            y = keep.tile([P, SLOTS, CHUNK], F32, name="y%d" % c)
            nc.scalar.activation(out=y[:], in_=acc[:], func=COPY, scale=SIXTEENTH)
            nc.sync.dma_start(out=out_rows[:, :, cols(c)], in_=y[:])
            return woven

        def store_codes(h):
            half = slice(HALF * h, HALF * (h + 1))
            nc.sync.dma_start(out=words_of(out_1)[:, half], in_=y_codes[:, half].bitcast(I32))

        zw0 = weights(0)
        zw1 = weights(1)
        quantize_chunk(zp, zp_plane, 0, zw0)
        quantize_chunk(zp, zp_plane, 1, zw1)
        sigs.append(scores(2))
        sigs.append(scores(3))
        yw0 = result(0)
        yw1 = result(1)
        zw2 = weights(2)
        quantize_chunk(y_codes, y_plane, 0, yw0)
        quantize_chunk(zp, zp_plane, 2, zw2)
        zw3 = weights(3)
        quantize_chunk(y_codes, y_plane, 1, yw1)
        quantize_chunk(zp, zp_plane, 3, zw3)
        store_codes(0)
        yw2 = result(2)
        yw3 = result(3)
        quantize_chunk(y_codes, y_plane, 2, yw2)
        quantize_chunk(y_codes, y_plane, 3, yw3)
        store_codes(1)
        for q in range(4):
            nc.sync.dma_start(out=out_2[0, 4 * q : 4 * q + 4, :].bitcast(I32), in_=y_plane[32 * q : 32 * q + 4, :].bitcast(I32))
